import numpy as np
import ml_dtypes


def mxq(x, axis, fmt="e4m3"):
    dtype, down = {"e4m3": (ml_dtypes.float8_e4m3fn, 7), "e5m2": (ml_dtypes.float8_e5m2, 14)}[fmt]
    v = np.moveaxis(np.asarray(x, np.float32).astype(ml_dtypes.bfloat16).astype(np.float64), axis, -1)
    blocks = v.reshape(v.shape[:-1] + (-1, 32))
    amax = np.abs(blocks).max(-1, keepdims=True)
    byte = np.maximum(np.where(amax > 0, np.frexp(amax)[1] - 1 + 127, 0) - down, 1)
    scale = np.exp2(byte - 127.0)
    codes = (blocks / scale).astype(np.float32).astype(dtype).astype(np.float64)
    return np.moveaxis((codes * scale).reshape(v.shape), -1, axis)


WIDE = False


def mx_kscale(k):
    if not WIDE:
        return np.ones(k)
    levels = np.array([10, -10, 5, -5, 0])
    if k % 512:
        return np.exp2(np.random.permutation(np.resize(levels, k // 32))).repeat(32)
    a = np.empty((k // 512, 16))
    for p in range(k // 512):
        a[p, :8] = np.random.permutation(np.resize(levels, 8))
        for g in range(8):
            far = levels[np.abs(levels - a[p, g]) >= 10]
            a[p, g + 8] = far[np.random.randint(len(far))]
    return np.exp2(a.ravel()).repeat(32)


def f64(x):
    return np.asarray(x).astype(np.float64)


def striped(idx):
    return np.tile(np.asarray(idx).reshape(-1, 16).T, (8, 1)).astype(np.uint16)


def unstriped(offs):
    return offs[:16].T.reshape(-1).astype(np.int64)


E2M1 = np.array([0.0, 0.5, 1.0, 1.5, 2.0, 3.0, 4.0, 6.0, -0.0, -0.5, -1.0, -1.5, -2.0, -3.0, -4.0, -6.0])


def pack_weight(w, fmt):
    k, n = w.shape
    w = f64(np.asarray(w, np.float32).astype(ml_dtypes.bfloat16)).reshape(k // 32, 32, n)
    amax = np.abs(w).max(1)
    if fmt == "e4m3":
        byte = np.frexp(amax)[1] - 1 + 127 - 7
    else:
        mant, ex = np.frexp(amax / 6.0)
        byte = np.where(mant > 0.5, ex, ex - 1) + 127
    byte = np.clip(np.where(amax > 0, byte, 1), 1, 254)
    scaled = (w * np.exp2(127.0 - byte)[:, None, :]).reshape(k, n).astype(np.float32)
    by_word = np.ascontiguousarray(scaled.reshape(k // 512, 128, 4, n).transpose(0, 1, 3, 2))
    if fmt == "e4m3":
        words = by_word.astype(ml_dtypes.float8_e4m3fn).view(np.uint8)
    else:
        c = by_word.astype(ml_dtypes.float4_e2m1fn).view(np.uint8) & 0xF
        words = (c[..., 0::2] | (c[..., 1::2] << 4)).reshape(k // 512, 128, 2 * n)
    return np.ascontiguousarray(words), np.ascontiguousarray(byte.astype(np.uint8).reshape(k // 512, 16, n))


def unpack_weight(words, scales, fmt):
    g, _, n = scales.shape
    words = np.ascontiguousarray(words).reshape(g, 128, n, -1)
    if fmt == "e4m3":
        vals = words.view(ml_dtypes.float8_e4m3fn).astype(np.float64)
    else:
        nib = np.empty((g, 128, n, 4), np.uint8)
        nib[..., 0::2] = words & 0xF
        nib[..., 1::2] = words >> 4
        vals = E2M1[nib]
    vals = vals * np.repeat(np.exp2(scales.astype(np.float64) - 127.0), 8, axis=1)[..., None]
    return vals.transpose(0, 1, 3, 2).reshape(g * 512, n)


B, N, T, D, NQ = 1, 512, 2048, 1024, 128


def setup_inputs():
    n = np.random.standard_normal
    idx = np.random.permutation(T)[:B * N]
    idx2 = np.random.permutation(1024)[:B * N]
    s = mx_kscale(D)[:, None]
    kp = pack_weight(n((D, T)) / s, "e2m1")
    cp = pack_weight(n((D, 1024)) / s, "e2m1")
    return {
        "uT": (n((B, D, NQ)) * s * (1.00 / np.sqrt(D))).astype(np.float32),
        "vT": (n((B, D, NQ)) * s * (1.00 / np.sqrt(D))).astype(np.float32),
        "k_words": np.ascontiguousarray(kp[0].reshape(1, 2, 128, T, 2).transpose(0, 2, 3, 1, 4)).reshape(1, 128, T, 4),
        "k_scales": kp[1],
        "c_words": np.ascontiguousarray(cp[0].reshape(1, 2, 128, 1024, 2).transpose(0, 2, 3, 1, 4)).reshape(1, 128, 1024, 4),
        "c_scales": cp[1],
        "offs": striped(idx),
        "offs2": striped(idx2),
    }


def reference(uT, vT, k_words, k_scales, c_words, c_scales, offs, offs2):
    idx = unstriped(offs)
    idx2 = unstriped(offs2)
    pick = lambda x, which: x[:, which].reshape(x.shape[0], B, -1).transpose(1, 0, 2)
    k = unpack_weight(k_words.reshape(1, 128, T, 2, 2).transpose(0, 3, 1, 2, 4).reshape(2, 128, 2 * T), k_scales, "e2m1")
    kg = pick(k, idx)
    c = unpack_weight(c_words.reshape(1, 128, 1024, 2, 2).transpose(0, 3, 1, 2, 4).reshape(2, 128, 2 * 1024), c_scales, "e2m1")
    cg = pick(c, idx2)
    uq = mxq(f64(uT), 1, "e4m3")
    vq = mxq(f64(vT), 1, "e4m3")
    a = (uq.transpose(0, 2, 1) @ kg) + (vq.transpose(0, 2, 1) @ cg)
    m = np.max(a, axis=-1, keepdims=True)
    e = np.exp(a - m)
    l = np.sum(e, axis=-1, keepdims=True)
    y = e / l
    return y

@@ -1,0 +1,145 @@
+from contextlib import ExitStack
+
+import concourse.mybir as mybir
+
+F32 = mybir.dt.float32
+BF16 = mybir.dt.bfloat16
+I32 = mybir.dt.int32
+U32 = mybir.dt.uint32
+U16 = mybir.dt.uint16
+U8 = mybir.dt.uint8
+FP8X4 = mybir.dt.float8_e4m3fn_x4
+FP4X4 = mybir.dt.float4_e2m1fn_x4
+ACT = mybir.ActivationFunctionType
+ALU = mybir.AluOpType
+
+P = 128
+PACK = 4
+K_PASS = P * PACK
+PASSES = 2
+NQ = 128
+SLOTS = 512
+FLOPS = 2 * 2 * NQ * SLOTS * PASSES * K_PASS
+
+
+def tile_attend_txlw_topk_kernel(tc, uT, vT, k_words, k_scales, c_words, c_scales, offs, offs2, out):
+    nc = tc.nc
+    with ExitStack() as ctx:
+        lists = ctx.enter_context(tc.tile_pool(name="lists", bufs=1))
+        sb = ctx.enter_context(tc.tile_pool(name="sb", bufs=1))
+        psum = ctx.enter_context(tc.psum_pool(name="psum", bufs=1))
+
+        k_list = lists.tile([P, SLOTS // 16], U16, name="k_list")
+        c_list = lists.tile([P, SLOTS // 16], U16, name="c_list")
+        k_cols = k_scales.shape[2]
+        c_cols = c_scales.shape[2]
+
+        ks_pool = sb.tile([P, k_cols], U8, name="ks_pool", align_bytes=64)
+        cs_pool = sb.tile([P, c_cols], U8, name="cs_pool", align_bytes=64)
+        kw_pool = sb.tile([P, k_cols], I32, name="kw_pool", align_bytes=64)
+        cw_pool = sb.tile([P, c_cols], I32, name="cw_pool", align_bytes=64)
+        planes = sb.tile([P, PASSES, 2, SLOTS], U8, name="planes", align_bytes=64)
+        picked_scales = sb.tile([P, 2, SLOTS], U8, name="picked_scales", align_bytes=64)
+
+        nc.sync.dma_start(k_list[:], offs)
+        nc.scalar.dma_start(ks_pool[0:32, :].bitcast(I32), k_scales.rearrange("o f n -> f o n").bitcast(I32))
+        nc.sync.dma_start(c_list[:], offs2)
+        nc.scalar.dma_start(cs_pool[0:32, :].bitcast(I32), c_scales.rearrange("o f n -> f o n").bitcast(I32))
+        nc.sync.dma_start(cw_pool[:], c_words[0].rearrange("p t b -> p (t b)").bitcast(I32))
+
+        def load_queries(src, o, name):
+            raw = sb.tile([P, PACK, NQ], F32, name=name)
+            nc.sync.dma_start(raw[:], src[0, o * K_PASS : (o + 1) * K_PASS, :].rearrange("(p j) q -> p j q", j=PACK))
+            return raw
+
+        v_raw = [load_queries(vT, o, "v_raw%d" % o) for o in range(PASSES)]
+        nc.sync.dma_start(kw_pool[:], k_words[0].rearrange("p t b -> p (t b)").bitcast(I32))
+        u_raw = [load_queries(uT, o, "u_raw%d" % o) for o in range(PASSES)]
+
+        for pool_tile in (ks_pool, cs_pool):
+            nc.vector.memset(pool_tile[32:64, :].bitcast(I32), 0)
+            nc.vector.memset(pool_tile[64:128, :].bitcast(I32), 0)
+        nc.vector.memset(planes[:].rearrange("p o s n -> p (o s n)").bitcast(I32), 0)
+
+        warm_in = sb.tile([P, 1], F32, name="warm_in")
+        warm_out = sb.tile([P, 1], F32, name="warm_out")
+        nc.gpsimd.memset(warm_in[:], 0.0)
+        nc.scalar.activation(warm_out[:], warm_in[:], ACT.Exp)
+
+        nc.vector.tensor_copy(picked_scales[:, 0, :], ks_pool[:].indirect(k_list[:]))
+        nc.vector.tensor_copy(picked_scales[:, 1, :], cs_pool[:].indirect(c_list[:]))
+        for quad in range(4):
+            nc.scalar.dma_start(
+                planes[32 * quad : 32 * quad + 4].rearrange("p o s n -> p o (s n)").bitcast(I32),
+                picked_scales[8 * quad : 8 * quad + 8].rearrange("p s n -> p (s n)").bitcast(I32),
+            )
+
+        def interleave(raw, name):
+            grouped = sb.tile([P, NQ, PACK], BF16, name=name, align_bytes=64)
+            nc.scalar.copy(
+                grouped[:].rearrange("p (c i) t -> p c t i", i=4),
+                raw[:].rearrange("p t (c i) -> p c t i", i=4),
+            )
+            return grouped
+
+        def quantize(grouped, name):
+            codes = sb.tile([P, NQ], U32, name=name + "_codes", align_bytes=64)
+            scales = sb.tile([P, NQ], U8, name=name + "_scales", align_bytes=64)
+            nc.vector.quantize_mx(
+                out=codes[:].bitcast(FP8X4), scales=scales[:], in_=grouped[:].rearrange("p q t -> p (q t)")
+            )
+            return codes, scales
+
+        def gather_words(pool_tile, slot_list, name):
+            picked = sb.tile([P, SLOTS], U32, name=name, align_bytes=64)
+            nc.vector.tensor_copy(picked[:], pool_tile[:].bitcast(U32).indirect(slot_list[:]))
+            return picked
+
+        def split(picked, o, name):
+            words = sb.tile([P, SLOTS], U16, name=name, align_bytes=64)
+            nc.vector.tensor_copy(words[:], picked[:].bitcast(U16).rearrange("p (n h) -> p h n", h=2)[:, o, :])
+            return words
+
+        scores = psum.tile([NQ, SLOTS], F32, name="scores")
+
+        def product(query, words, o, table, start, stop):
+            nc.tensor.matmul_mx(
+                out=scores[:],
+                lhsT=query[0][:].bitcast(FP8X4),
+                lhsT_scale=query[1][:],
+                rhs=words[:].bitcast(FP4X4),
+                rhs_scale=planes[:, o, table, :],
+                start=start,
+                stop=stop,
+            )
+
+        v_grouped = [interleave(v_raw[o], "v_grouped%d" % o) for o in range(PASSES)]
+        u_grouped = [interleave(u_raw[o], "u_grouped%d" % o) for o in range(PASSES)]
+
+        c_picked = gather_words(cw_pool, c_list, "c_picked")
+        vq0 = quantize(v_grouped[0], "v0")
+        c0 = split(c_picked, 0, "c0")
+        vq1 = quantize(v_grouped[1], "v1")
+        c1 = split(c_picked, 1, "c1")
+        product(vq0, c0, 0, 1, True, False)
+        product(vq1, c1, 1, 1, False, False)
+        k_picked = gather_words(kw_pool, k_list, "k_picked")
+        uq0 = quantize(u_grouped[0], "u0")
+        k0 = split(k_picked, 0, "k0")
+        product(uq0, k0, 0, 0, False, False)
+        k1 = split(k_picked, 1, "k1")
+        uq1 = quantize(u_grouped[1], "u1")
+        product(uq1, k1, 1, 0, False, True)
+
+        neg_max = sb.tile([P, 1], F32, name="neg_max")
+        nc.vector.tensor_reduce(neg_max[:], scores[:], mybir.AxisListType.X, ALU.max, negate=True)
+        weights = sb.tile([P, SLOTS], F32, name="weights")
+        row_sum = sb.tile([P, 1], F32, name="row_sum")
+        nc.scalar.activation(weights[:], scores[:], ACT.Exp, bias=neg_max[:], scale=1.0, accum_out=row_sum[:])
+        inv_sum = sb.tile([P, 1], F32, name="inv_sum")
+        nc.vector.reciprocal(inv_sum[:], row_sum[:])
+        half = SLOTS // 2
+        for h, queue in enumerate((nc.sync, nc.scalar)):
+            result = sb.tile([P, half], F32, name="result%d" % h)
+            nc.vector.tensor_scalar(result[:], weights[:, h * half : (h + 1) * half], inv_sum[:], None, ALU.mult)
+            queue.dma_start(out[0, :, h * half : (h + 1) * half], result[:])

@@ -34,102 +34,107 @@ def tile_attend_txlw_topk_kernel(tc, uT, vT, k_words, k_scales, c_words, c_scale
         k_cols = k_scales.shape[2]
         c_cols = c_scales.shape[2]
 
-        ks_pool = sb.tile([P, k_cols], U8, name="ks_pool", align_bytes=64)
+        ks_pool = sb.tile([P, k_cols], U8, name="ks_pool", tag="k_scales_then_u", align_bytes=64)
         cs_pool = sb.tile([P, c_cols], U8, name="cs_pool", align_bytes=64)
         kw_pool = sb.tile([P, k_cols], I32, name="kw_pool", align_bytes=64)
         cw_pool = sb.tile([P, c_cols], I32, name="cw_pool", align_bytes=64)
         planes = sb.tile([P, PASSES, 2, SLOTS], U8, name="planes", align_bytes=64)
         picked_scales = sb.tile([P, 2, SLOTS], U8, name="picked_scales", align_bytes=64)
 
-        nc.sync.dma_start(k_list[:], offs)
-        nc.scalar.dma_start(ks_pool[0:32, :].bitcast(I32), k_scales.rearrange("o f n -> f o n").bitcast(I32))
         nc.sync.dma_start(c_list[:], offs2)
-        nc.scalar.dma_start(cs_pool[0:32, :].bitcast(I32), c_scales.rearrange("o f n -> f o n").bitcast(I32))
-        nc.sync.dma_start(cw_pool[:], c_words[0].rearrange("p t b -> p (t b)").bitcast(I32))
+        nc.scalar.dma_start(cs_pool[96:128, :].bitcast(I32), c_scales.rearrange("o f n -> f o n").bitcast(I32))
+        nc.sync.dma_start(k_list[:], offs)
+        nc.scalar.dma_start(ks_pool[96:128, :].bitcast(I32), k_scales.rearrange("o f n -> f o n").bitcast(I32))
+        nc.scalar.dma_start(cw_pool[:], c_words[0].rearrange("p t b -> p (t b)").bitcast(I32))
 
-        def load_queries(src, o, name):
-            raw = sb.tile([P, PACK, NQ], F32, name=name)
-            nc.sync.dma_start(raw[:], src[0, o * K_PASS : (o + 1) * K_PASS, :].rearrange("(p j) q -> p j q", j=PACK))
+        def load_queries(src, o, tag):
+            raw = sb.tile([P, PACK, NQ], F32, name=tag + "_raw", tag=tag, align_bytes=64)
+            rows = src[0, o * K_PASS : (o + 1) * K_PASS, :]
+            nc.sync.dma_start(raw[:], rows.rearrange("(p j) q -> p j q", j=PACK))
             return raw
 
-        v_raw = [load_queries(vT, o, "v_raw%d" % o) for o in range(PASSES)]
+        v_raw = [load_queries(vT, 0, "v0"), load_queries(vT, 1, "v1")]
         nc.sync.dma_start(kw_pool[:], k_words[0].rearrange("p t b -> p (t b)").bitcast(I32))
-        u_raw = [load_queries(uT, o, "u_raw%d" % o) for o in range(PASSES)]
-
-        for pool_tile in (ks_pool, cs_pool):
-            nc.vector.memset(pool_tile[32:64, :].bitcast(I32), 0)
-            nc.vector.memset(pool_tile[64:128, :].bitcast(I32), 0)
-        nc.vector.memset(planes[:].rearrange("p o s n -> p (o s n)").bitcast(I32), 0)
+        u_raw = [load_queries(uT, 0, "u0")]
 
         warm_in = sb.tile([P, 1], F32, name="warm_in")
         warm_out = sb.tile([P, 1], F32, name="warm_out")
         nc.gpsimd.memset(warm_in[:], 0.0)
+        nc.vector.memset(cs_pool[0:96, :].bitcast(I32), 0)
+        nc.gpsimd.memset(ks_pool[0:96, :].bitcast(I32), 0)
+        nc.gpsimd.memset(planes[:].rearrange("p o s n -> p (o s n)").bitcast(I32), 0)
         nc.scalar.activation(warm_out[:], warm_in[:], ACT.Exp)
 
-        nc.vector.tensor_copy(picked_scales[:, 0, :], ks_pool[:].indirect(k_list[:]))
         nc.vector.tensor_copy(picked_scales[:, 1, :], cs_pool[:].indirect(c_list[:]))
+        nc.vector.tensor_copy(picked_scales[:, 0, :], ks_pool[:].indirect(k_list[:]))
         for quad in range(4):
-            nc.scalar.dma_start(
+            nc.sync.dma_start(
                 planes[32 * quad : 32 * quad + 4].rearrange("p o s n -> p o (s n)").bitcast(I32),
-                picked_scales[8 * quad : 8 * quad + 8].rearrange("p s n -> p (s n)").bitcast(I32),
+                picked_scales[96 + 8 * quad : 96 + 8 * quad + 8].rearrange("p s n -> p (s n)").bitcast(I32),
             )
+        u_raw.append(load_queries(uT, 1, "k_scales_then_u"))
 
-        def interleave(raw, name):
-            grouped = sb.tile([P, NQ, PACK], BF16, name=name, align_bytes=64)
+        def interleave(grouped, raw):
             nc.scalar.copy(
-                grouped[:].rearrange("p (c i) t -> p c t i", i=4),
+                grouped.rearrange("p (c i) t -> p c t i", i=4),
                 raw[:].rearrange("p t (c i) -> p c t i", i=4),
             )
-            return grouped
 
-        def quantize(grouped, name):
-            codes = sb.tile([P, NQ], U32, name=name + "_codes", align_bytes=64)
-            scales = sb.tile([P, NQ], U8, name=name + "_scales", align_bytes=64)
-            nc.vector.quantize_mx(
-                out=codes[:].bitcast(FP8X4), scales=scales[:], in_=grouped[:].rearrange("p q t -> p (q t)")
-            )
+        def quantize(grouped, width, name):
+            codes = sb.tile([P, width], U32, name=name + "_codes", align_bytes=64)
+            scales = sb.tile([P, width], U8, name=name + "_scales", align_bytes=64)
+            nc.vector.quantize_mx(out=codes[:].bitcast(FP8X4), scales=scales[:], in_=grouped)
             return codes, scales
-
-        def gather_words(pool_tile, slot_list, name):
-            picked = sb.tile([P, SLOTS], U32, name=name, align_bytes=64)
-            nc.vector.tensor_copy(picked[:], pool_tile[:].bitcast(U32).indirect(slot_list[:]))
-            return picked
-
-        def split(picked, o, name):
-            words = sb.tile([P, SLOTS], U16, name=name, align_bytes=64)
-            nc.vector.tensor_copy(words[:], picked[:].bitcast(U16).rearrange("p (n h) -> p h n", h=2)[:, o, :])
-            return words
 
         scores = psum.tile([NQ, SLOTS], F32, name="scores")
 
-        def product(query, words, o, table, start, stop):
+        def product(codes, scales, words, o, table, start, stop):
             nc.tensor.matmul_mx(
                 out=scores[:],
-                lhsT=query[0][:].bitcast(FP8X4),
-                lhsT_scale=query[1][:],
-                rhs=words[:].bitcast(FP4X4),
+                lhsT=codes.bitcast(FP8X4),
+                lhsT_scale=scales,
+                rhs=words.bitcast(FP4X4),
                 rhs_scale=planes[:, o, table, :],
                 start=start,
                 stop=stop,
             )
 
-        v_grouped = [interleave(v_raw[o], "v_grouped%d" % o) for o in range(PASSES)]
-        u_grouped = [interleave(u_raw[o], "u_grouped%d" % o) for o in range(PASSES)]
+        v_grouped = sb.tile([P, PASSES, NQ, PACK], BF16, name="v_grouped", align_bytes=64)
+        u_grouped = [
+            sb.tile([P, NQ, PACK], BF16, name="u_grouped%d" % o, tag="u_grouped%d" % o, align_bytes=64)
+            for o in range(PASSES)
+        ]
+        for o in range(PASSES):
+            interleave(v_grouped[:, o], v_raw[o])
+        for o in range(PASSES):
+            interleave(u_grouped[o][:], u_raw[o])
 
-        c_picked = gather_words(cw_pool, c_list, "c_picked")
-        vq0 = quantize(v_grouped[0], "v0")
-        c0 = split(c_picked, 0, "c0")
-        vq1 = quantize(v_grouped[1], "v1")
-        c1 = split(c_picked, 1, "c1")
-        product(vq0, c0, 0, 1, True, False)
-        product(vq1, c1, 1, 1, False, False)
-        k_picked = gather_words(kw_pool, k_list, "k_picked")
-        uq0 = quantize(u_grouped[0], "u0")
-        k0 = split(k_picked, 0, "k0")
-        product(uq0, k0, 0, 0, False, False)
-        k1 = split(k_picked, 1, "k1")
-        uq1 = quantize(u_grouped[1], "u1")
-        product(uq1, k1, 1, 0, False, True)
+        c_picked = sb.tile([P, SLOTS], U32, name="c_picked", align_bytes=64)
+        nc.vector.tensor_copy(c_picked[:], cw_pool[:].bitcast(U32).indirect(c_list[:]))
+        v_codes, v_scales = quantize(v_grouped[:].rearrange("p o q t -> p (o q t)"), PASSES * NQ, "v")
+        c_pass = sb.tile([P, PASSES, SLOTS], U16, name="c_pass", align_bytes=64)
+        nc.vector.tensor_copy(c_pass[:], c_picked[:].bitcast(U16).rearrange("p (n h) -> p h n", h=2))
+        for o in range(PASSES):
+            cols = slice(o * NQ, (o + 1) * NQ)
+            product(v_codes[:, cols], v_scales[:, cols], c_pass[:, o, :], o, 1, o == 0, False)
+
+        half = SLOTS // 2
+        k_picked = sb.tile([P, SLOTS], U32, name="k_picked", align_bytes=64)
+        for h in range(2):
+            nc.vector.tensor_copy(
+                k_picked[:, h * half : (h + 1) * half],
+                kw_pool[:].bitcast(U32).indirect(k_list[:, h * half // 16 : (h + 1) * half // 16]),
+            )
+        k_halves = k_picked[:].bitcast(U16).rearrange("p (n h) -> p h n", h=2)
+        k0 = sb.tile([P, SLOTS], U16, name="k0", align_bytes=64)
+        for h in range(2):
+            nc.vector.tensor_copy(k0[:, h * half : (h + 1) * half], k_halves[:, 0, h * half : (h + 1) * half])
+        u0_codes, u0_scales = quantize(u_grouped[0][:].rearrange("p q t -> p (q t)"), NQ, "u0")
+        product(u0_codes[:], u0_scales[:], k0[:], 0, 0, False, False)
+        k1 = sb.tile([P, SLOTS], U16, name="k1", tag="u_grouped0", align_bytes=64)
+        nc.vector.tensor_copy(k1[:], k_halves[:, 1, :])
+        u1_codes, u1_scales = quantize(u_grouped[1][:].rearrange("p q t -> p (q t)"), NQ, "u1")
+        product(u1_codes[:], u1_scales[:], k1[:], 1, 0, False, True)
 
         neg_max = sb.tile([P, 1], F32, name="neg_max")
         nc.vector.tensor_reduce(neg_max[:], scores[:], mybir.AxisListType.X, ALU.max, negate=True)
@@ -138,7 +143,6 @@ def tile_attend_txlw_topk_kernel(tc, uT, vT, k_words, k_scales, c_words, c_scale
         nc.scalar.activation(weights[:], scores[:], ACT.Exp, bias=neg_max[:], scale=1.0, accum_out=row_sum[:])
         inv_sum = sb.tile([P, 1], F32, name="inv_sum")
         nc.vector.reciprocal(inv_sum[:], row_sum[:])
-        half = SLOTS // 2
         for h, queue in enumerate((nc.sync, nc.scalar)):
             result = sb.tile([P, half], F32, name="result%d" % h)
             nc.vector.tensor_scalar(result[:], weights[:, h * half : (h + 1) * half], inv_sum[:], None, ALU.mult)

@@ -34,18 +34,16 @@ def tile_attend_txlw_topk_kernel(tc, uT, vT, k_words, k_scales, c_words, c_scale
         k_cols = k_scales.shape[2]
         c_cols = c_scales.shape[2]
 
-        ks_pool = sb.tile([P, k_cols], U8, name="ks_pool", tag="k_scales_then_u", align_bytes=64)
+        ks_pool = sb.tile([P, k_cols], U8, name="ks_pool", align_bytes=64)
         cs_pool = sb.tile([P, c_cols], U8, name="cs_pool", align_bytes=64)
         kw_pool = sb.tile([P, k_cols], I32, name="kw_pool", align_bytes=64)
         cw_pool = sb.tile([P, c_cols], I32, name="cw_pool", align_bytes=64)
-        planes = sb.tile([P, PASSES, 2, SLOTS], U8, name="planes", align_bytes=64)
         picked_scales = sb.tile([P, 2, SLOTS], U8, name="picked_scales", align_bytes=64)
 
         nc.sync.dma_start(c_list[:], offs2)
         nc.scalar.dma_start(cs_pool[96:128, :].bitcast(I32), c_scales.rearrange("o f n -> f o n").bitcast(I32))
         nc.sync.dma_start(k_list[:], offs)
         nc.scalar.dma_start(ks_pool[96:128, :].bitcast(I32), k_scales.rearrange("o f n -> f o n").bitcast(I32))
-        nc.scalar.dma_start(cw_pool[:], c_words[0].rearrange("p t b -> p (t b)").bitcast(I32))
 
         def load_queries(src, o, tag):
             raw = sb.tile([P, PACK, NQ], F32, name=tag + "_raw", tag=tag, align_bytes=64)
@@ -54,25 +52,12 @@ def tile_attend_txlw_topk_kernel(tc, uT, vT, k_words, k_scales, c_words, c_scale
             return raw
 
         v_raw = [load_queries(vT, 0, "v0"), load_queries(vT, 1, "v1")]
+        nc.sync.dma_start(cw_pool[:], c_words[0].rearrange("p t b -> p (t b)").bitcast(I32))
         nc.sync.dma_start(kw_pool[:], k_words[0].rearrange("p t b -> p (t b)").bitcast(I32))
-        u_raw = [load_queries(uT, 0, "u0")]
+        u_raw = [load_queries(uT, 0, "u0"), load_queries(uT, 1, "u1")]
 
-        warm_in = sb.tile([P, 1], F32, name="warm_in")
-        warm_out = sb.tile([P, 1], F32, name="warm_out")
-        nc.gpsimd.memset(warm_in[:], 0.0)
         nc.vector.memset(cs_pool[0:96, :].bitcast(I32), 0)
         nc.gpsimd.memset(ks_pool[0:96, :].bitcast(I32), 0)
-        nc.gpsimd.memset(planes[:].rearrange("p o s n -> p (o s n)").bitcast(I32), 0)
-        nc.scalar.activation(warm_out[:], warm_in[:], ACT.Exp)
-
-        nc.vector.tensor_copy(picked_scales[:, 1, :], cs_pool[:].indirect(c_list[:]))
-        nc.vector.tensor_copy(picked_scales[:, 0, :], ks_pool[:].indirect(k_list[:]))
-        for quad in range(4):
-            nc.sync.dma_start(
-                planes[32 * quad : 32 * quad + 4].rearrange("p o s n -> p o (s n)").bitcast(I32),
-                picked_scales[96 + 8 * quad : 96 + 8 * quad + 8].rearrange("p s n -> p (s n)").bitcast(I32),
-            )
-        u_raw.append(load_queries(uT, 1, "k_scales_then_u"))
 
         def interleave(grouped, raw):
             nc.scalar.copy(
@@ -88,13 +73,13 @@ def tile_attend_txlw_topk_kernel(tc, uT, vT, k_words, k_scales, c_words, c_scale
 
         scores = psum.tile([NQ, SLOTS], F32, name="scores")
 
-        def product(codes, scales, words, o, table, start, stop):
+        def product(codes, scales, words, o, table, slots, start, stop):
             nc.tensor.matmul_mx(
-                out=scores[:],
+                out=scores[:, slots],
                 lhsT=codes.bitcast(FP8X4),
                 lhsT_scale=scales,
                 rhs=words.bitcast(FP4X4),
-                rhs_scale=planes[:, o, table, :],
+                rhs_scale=planes[:, o, table, slots],
                 start=start,
                 stop=stop,
             )
@@ -106,9 +91,19 @@ def tile_attend_txlw_topk_kernel(tc, uT, vT, k_words, k_scales, c_words, c_scale
         ]
         for o in range(PASSES):
             interleave(v_grouped[:, o], v_raw[o])
+
+        nc.vector.tensor_copy(picked_scales[:, 1, :], cs_pool[:].indirect(c_list[:]))
+        nc.vector.tensor_copy(picked_scales[:, 0, :], ks_pool[:].indirect(k_list[:]))
+        planes = sb.tile([P, PASSES, 2, SLOTS], U8, name="planes", tag="v1", align_bytes=64)
+        for quad in range(4):
+            nc.scalar.dma_start(
+                planes[32 * quad : 32 * quad + 4].rearrange("p o s n -> p o (s n)").bitcast(I32),
+                picked_scales[96 + 8 * quad : 96 + 8 * quad + 8].rearrange("p s n -> p (s n)").bitcast(I32),
+            )
         for o in range(PASSES):
             interleave(u_grouped[o][:], u_raw[o])
 
+        every = slice(0, SLOTS)
         c_picked = sb.tile([P, SLOTS], U32, name="c_picked", align_bytes=64)
         nc.vector.tensor_copy(c_picked[:], cw_pool[:].bitcast(U32).indirect(c_list[:]))
         v_codes, v_scales = quantize(v_grouped[:].rearrange("p o q t -> p (o q t)"), PASSES * NQ, "v")
@@ -116,7 +111,7 @@ def tile_attend_txlw_topk_kernel(tc, uT, vT, k_words, k_scales, c_words, c_scale
         nc.vector.tensor_copy(c_pass[:], c_picked[:].bitcast(U16).rearrange("p (n h) -> p h n", h=2))
         for o in range(PASSES):
             cols = slice(o * NQ, (o + 1) * NQ)
-            product(v_codes[:, cols], v_scales[:, cols], c_pass[:, o, :], o, 1, o == 0, False)
+            product(v_codes[:, cols], v_scales[:, cols], c_pass[:, o, :], o, 1, every, o == 0, False)
 
         half = SLOTS // 2
         k_picked = sb.tile([P, SLOTS], U32, name="k_picked", align_bytes=64)
@@ -126,15 +121,14 @@ def tile_attend_txlw_topk_kernel(tc, uT, vT, k_words, k_scales, c_words, c_scale
                 kw_pool[:].bitcast(U32).indirect(k_list[:, h * half // 16 : (h + 1) * half // 16]),
             )
         k_halves = k_picked[:].bitcast(U16).rearrange("p (n h) -> p h n", h=2)
-        k0 = sb.tile([P, SLOTS], U16, name="k0", align_bytes=64)
-        for h in range(2):
-            nc.vector.tensor_copy(k0[:, h * half : (h + 1) * half], k_halves[:, 0, h * half : (h + 1) * half])
-        u0_codes, u0_scales = quantize(u_grouped[0][:].rearrange("p q t -> p (q t)"), NQ, "u0")
-        product(u0_codes[:], u0_scales[:], k0[:], 0, 0, False, False)
-        k1 = sb.tile([P, SLOTS], U16, name="k1", tag="u_grouped0", align_bytes=64)
-        nc.vector.tensor_copy(k1[:], k_halves[:, 1, :])
-        u1_codes, u1_scales = quantize(u_grouped[1][:].rearrange("p q t -> p (q t)"), NQ, "u1")
-        product(u1_codes[:], u1_scales[:], k1[:], 1, 0, False, True)
+        k_pass = sb.tile([P, PASSES, SLOTS], U16, name="k_pass", align_bytes=64)
+        for o in range(PASSES):
+            u_codes, u_scales = quantize(u_grouped[o][:].rearrange("p q t -> p (q t)"), NQ, "u%d" % o)
+            for h in range(2):
+                nc.vector.tensor_copy(k_pass[:, o, h * half : (h + 1) * half], k_halves[:, o, h * half : (h + 1) * half])
+                for g in range(2):
+                    slots = slice(h * half + g * NQ, h * half + (g + 1) * NQ)
+                    product(u_codes[:], u_scales[:], k_pass[:, o, slots], o, 0, slots, False, (o, h, g) == (1, 1, 1))
 
         neg_max = sb.tile([P, 1], F32, name="neg_max")
         nc.vector.tensor_reduce(neg_max[:], scores[:], mybir.AxisListType.X, ALU.max, negate=True)
@@ -143,7 +137,10 @@ def tile_attend_txlw_topk_kernel(tc, uT, vT, k_words, k_scales, c_words, c_scale
         nc.scalar.activation(weights[:], scores[:], ACT.Exp, bias=neg_max[:], scale=1.0, accum_out=row_sum[:])
         inv_sum = sb.tile([P, 1], F32, name="inv_sum")
         nc.vector.reciprocal(inv_sum[:], row_sum[:])
-        for h, queue in enumerate((nc.sync, nc.scalar)):
-            result = sb.tile([P, half], F32, name="result%d" % h)
-            nc.vector.tensor_scalar(result[:], weights[:, h * half : (h + 1) * half], inv_sum[:], None, ALU.mult)
-            queue.dma_start(out[0, :, h * half : (h + 1) * half], result[:])
+        split = 320
+        left = sb.tile([P, split], F32, name="left")
+        right = sb.tile([P, SLOTS - split], F32, name="right")
+        nc.vector.tensor_scalar(left[:], weights[:, :split], inv_sum[:], None, ALU.mult)
+        nc.sync.dma_start(out[0, :, :split], left[:])
+        nc.scalar.activation(right[:], weights[:, split:], ACT.Copy, scale=inv_sum[:])
+        nc.scalar.dma_start(out[0, :, split:], right[:])

@@ -27,6 +27,7 @@ def tile_attend_txlw_topk_kernel(tc, uT, vT, k_words, k_scales, c_words, c_scale
     with ExitStack() as ctx:
         lists = ctx.enter_context(tc.tile_pool(name="lists", bufs=1))
         sb = ctx.enter_context(tc.tile_pool(name="sb", bufs=1))
+        held = ctx.enter_context(tc.tile_pool(name="held", bufs=1))
         psum = ctx.enter_context(tc.psum_pool(name="psum", bufs=1))
 
         k_list = lists.tile([P, SLOTS // 16], U16, name="k_list")
@@ -44,17 +45,18 @@ def tile_attend_txlw_topk_kernel(tc, uT, vT, k_words, k_scales, c_words, c_scale
         nc.scalar.dma_start(cs_pool[96:128, :].bitcast(I32), c_scales.rearrange("o f n -> f o n").bitcast(I32))
         nc.sync.dma_start(k_list[:], offs)
         nc.scalar.dma_start(ks_pool[96:128, :].bitcast(I32), k_scales.rearrange("o f n -> f o n").bitcast(I32))
+        nc.scalar.dma_start(cw_pool[:], c_words[0].rearrange("p t b -> p (t b)").bitcast(I32))
 
-        def load_queries(src, o, tag):
-            raw = sb.tile([P, PACK, NQ], F32, name=tag + "_raw", tag=tag, align_bytes=64)
+        def load_queries(src, o, raw, queue):
             rows = src[0, o * K_PASS : (o + 1) * K_PASS, :]
-            nc.sync.dma_start(raw[:], rows.rearrange("(p j) q -> p j q", j=PACK))
+            queue.dma_start(raw[:], rows.rearrange("(p j) q -> p j q", j=PACK))
             return raw
 
-        v_raw = [load_queries(vT, 0, "v0"), load_queries(vT, 1, "v1")]
-        nc.sync.dma_start(cw_pool[:], c_words[0].rearrange("p t b -> p (t b)").bitcast(I32))
+        v_raw = [
+            load_queries(vT, 0, sb.tile([P, PACK, NQ], F32, name="v_raw0", align_bytes=64), nc.sync),
+            load_queries(vT, 1, held.tile([P, PACK, NQ], F32, name="v_raw1", align_bytes=64, offset=1024), nc.sync),
+        ]
         nc.sync.dma_start(kw_pool[:], k_words[0].rearrange("p t b -> p (t b)").bitcast(I32))
-        u_raw = [load_queries(uT, 0, "u0"), load_queries(uT, 1, "u1")]
 
         nc.vector.memset(cs_pool[0:96, :].bitcast(I32), 0)
         nc.gpsimd.memset(ks_pool[0:96, :].bitcast(I32), 0)
@@ -94,12 +96,16 @@ def tile_attend_txlw_topk_kernel(tc, uT, vT, k_words, k_scales, c_words, c_scale
 
         nc.vector.tensor_copy(picked_scales[:, 1, :], cs_pool[:].indirect(c_list[:]))
         nc.vector.tensor_copy(picked_scales[:, 0, :], ks_pool[:].indirect(k_list[:]))
-        planes = sb.tile([P, PASSES, 2, SLOTS], U8, name="planes", tag="v1", align_bytes=64)
-        for quad in range(4):
-            nc.scalar.dma_start(
+        planes = sb.tile([P, PASSES, 2, SLOTS], U8, name="planes", align_bytes=64)
+        for quad in (0, 2, 1, 3):
+            nc.sync.dma_start(
                 planes[32 * quad : 32 * quad + 4].rearrange("p o s n -> p o (s n)").bitcast(I32),
                 picked_scales[96 + 8 * quad : 96 + 8 * quad + 8].rearrange("p s n -> p (s n)").bitcast(I32),
             )
+        u_raw = [
+            load_queries(uT, o, held.tile([P, PACK, NQ], F32, name="u_raw%d" % o, align_bytes=64, offset=2048 * o), nc.scalar)
+            for o in range(PASSES)
+        ]
         for o in range(PASSES):
             interleave(u_grouped[o][:], u_raw[o])
 
@@ -121,14 +127,15 @@ def tile_attend_txlw_topk_kernel(tc, uT, vT, k_words, k_scales, c_words, c_scale
                 kw_pool[:].bitcast(U32).indirect(k_list[:, h * half // 16 : (h + 1) * half // 16]),
             )
         k_halves = k_picked[:].bitcast(U16).rearrange("p (n h) -> p h n", h=2)
-        k_pass = sb.tile([P, PASSES, SLOTS], U16, name="k_pass", align_bytes=64)
-        for o in range(PASSES):
-            u_codes, u_scales = quantize(u_grouped[o][:].rearrange("p q t -> p (q t)"), NQ, "u%d" % o)
-            for h in range(2):
-                nc.vector.tensor_copy(k_pass[:, o, h * half : (h + 1) * half], k_halves[:, o, h * half : (h + 1) * half])
-                for g in range(2):
-                    slots = slice(h * half + g * NQ, h * half + (g + 1) * NQ)
-                    product(u_codes[:], u_scales[:], k_pass[:, o, slots], o, 0, slots, False, (o, h, g) == (1, 1, 1))
+        k0 = sb.tile([P, SLOTS], U16, name="k0", align_bytes=64)
+        for h in range(2):
+            nc.vector.tensor_copy(k0[:, h * half : (h + 1) * half], k_halves[:, 0, h * half : (h + 1) * half])
+        u0_codes, u0_scales = quantize(u_grouped[0][:].rearrange("p q t -> p (q t)"), NQ, "u0")
+        product(u0_codes[:], u0_scales[:], k0[:], 0, 0, every, False, False)
+        k1 = sb.tile([P, SLOTS], U16, name="k1", tag="u_grouped0", align_bytes=64)
+        nc.vector.tensor_copy(k1[:], k_halves[:, 1, :])
+        u1_codes, u1_scales = quantize(u_grouped[1][:].rearrange("p q t -> p (q t)"), NQ, "u1")
+        product(u1_codes[:], u1_scales[:], k1[:], 1, 0, every, False, True)
 
         neg_max = sb.tile([P, 1], F32, name="neg_max")
         nc.vector.tensor_reduce(neg_max[:], scores[:], mybir.AxisListType.X, ALU.max, negate=True)

@@ -43,7 +43,6 @@ def tile_attend_txlw_topk_kernel(tc, uT, vT, k_words, k_scales, c_words, c_scale
 
         nc.sync.dma_start(c_list[:], offs2)
         nc.scalar.dma_start(cs_pool[96:128, :].bitcast(I32), c_scales.rearrange("o f n -> f o n").bitcast(I32))
-        nc.sync.dma_start(k_list[:], offs)
         nc.scalar.dma_start(ks_pool[96:128, :].bitcast(I32), k_scales.rearrange("o f n -> f o n").bitcast(I32))
         nc.scalar.dma_start(cw_pool[:], c_words[0].rearrange("p t b -> p (t b)").bitcast(I32))
 
@@ -54,8 +53,10 @@ def tile_attend_txlw_topk_kernel(tc, uT, vT, k_words, k_scales, c_words, c_scale
 
         v_raw = [
             load_queries(vT, 0, sb.tile([P, PACK, NQ], F32, name="v_raw0", align_bytes=64), nc.sync),
-            load_queries(vT, 1, held.tile([P, PACK, NQ], F32, name="v_raw1", align_bytes=64, offset=1024), nc.sync),
         ]
+        nc.sync.dma_start(k_list[:], offs)
+        v1_room = held.tile([P, 2 * PACK, NQ], F32, name="v1_room", align_bytes=64, offset=1024)
+        v_raw.append(load_queries(vT, 1, v1_room[:, :PACK], nc.sync))
         nc.sync.dma_start(kw_pool[:], k_words[0].rearrange("p t b -> p (t b)").bitcast(I32))
 
         nc.vector.memset(cs_pool[0:96, :].bitcast(I32), 0)
@@ -103,7 +104,7 @@ def tile_attend_txlw_topk_kernel(tc, uT, vT, k_words, k_scales, c_words, c_scale
                 picked_scales[96 + 8 * quad : 96 + 8 * quad + 8].rearrange("p s n -> p (s n)").bitcast(I32),
             )
         u_raw = [
-            load_queries(uT, o, held.tile([P, PACK, NQ], F32, name="u_raw%d" % o, align_bytes=64, offset=2048 * o), nc.scalar)
+            load_queries(uT, o, held.tile([P, PACK, NQ], F32, name="u_raw%d" % o, align_bytes=64, offset=4096 * o), nc.scalar)
             for o in range(PASSES)
         ]
         for o in range(PASSES):
@@ -113,29 +114,40 @@ def tile_attend_txlw_topk_kernel(tc, uT, vT, k_words, k_scales, c_words, c_scale
         c_picked = sb.tile([P, SLOTS], U32, name="c_picked", align_bytes=64)
         nc.vector.tensor_copy(c_picked[:], cw_pool[:].bitcast(U32).indirect(c_list[:]))
         v_codes, v_scales = quantize(v_grouped[:].rearrange("p o q t -> p (o q t)"), PASSES * NQ, "v")
-        c_pass = sb.tile([P, PASSES, SLOTS], U16, name="c_pass", align_bytes=64)
+        c_pass = held.tile([P, PASSES, SLOTS], U16, name="c_pass", align_bytes=64, offset=2048)
         nc.vector.tensor_copy(c_pass[:], c_picked[:].bitcast(U16).rearrange("p (n h) -> p h n", h=2))
+        warm = psum.tile([NQ, SLOTS], F32, name="warm")
+        nc.tensor.matmul_mx(
+            out=warm[:],
+            lhsT=v_codes[:, :NQ].bitcast(FP8X4),
+            lhsT_scale=v_scales[:, :NQ],
+            rhs=c_picked[:, : SLOTS // 2].bitcast(U16).bitcast(FP4X4),
+            rhs_scale=picked_scales[:, 1, :],
+            start=True,
+            stop=True,
+        )
         for o in range(PASSES):
             cols = slice(o * NQ, (o + 1) * NQ)
             product(v_codes[:, cols], v_scales[:, cols], c_pass[:, o, :], o, 1, every, o == 0, False)
 
         half = SLOTS // 2
-        k_picked = sb.tile([P, SLOTS], U32, name="k_picked", align_bytes=64)
+        k_pass = sb.tile([P, PASSES, SLOTS], U16, name="k_pass", align_bytes=64)
+        k_picked = [sb.tile([P, half], U32, name="k_picked%d" % h, tag="k_picked%d" % h, align_bytes=64) for h in range(2)]
         for h in range(2):
             nc.vector.tensor_copy(
-                k_picked[:, h * half : (h + 1) * half],
+                k_picked[h][:],
                 kw_pool[:].bitcast(U32).indirect(k_list[:, h * half // 16 : (h + 1) * half // 16]),
             )
-        k_halves = k_picked[:].bitcast(U16).rearrange("p (n h) -> p h n", h=2)
-        k0 = sb.tile([P, SLOTS], U16, name="k0", align_bytes=64)
         for h in range(2):
-            nc.vector.tensor_copy(k0[:, h * half : (h + 1) * half], k_halves[:, 0, h * half : (h + 1) * half])
-        u0_codes, u0_scales = quantize(u_grouped[0][:].rearrange("p q t -> p (q t)"), NQ, "u0")
-        product(u0_codes[:], u0_scales[:], k0[:], 0, 0, every, False, False)
-        k1 = sb.tile([P, SLOTS], U16, name="k1", tag="u_grouped0", align_bytes=64)
-        nc.vector.tensor_copy(k1[:], k_halves[:, 1, :])
-        u1_codes, u1_scales = quantize(u_grouped[1][:].rearrange("p q t -> p (q t)"), NQ, "u1")
-        product(u1_codes[:], u1_scales[:], k1[:], 1, 0, every, False, True)
+            nc.vector.tensor_copy(
+                k_pass[:, :, h * half : (h + 1) * half],
+                k_picked[h][:].bitcast(U16).rearrange("p (n h) -> p h n", h=2),
+            )
+        for o in range(PASSES):
+            u_codes, u_scales = quantize(u_grouped[o][:].rearrange("p q t -> p (q t)"), NQ, "u%d" % o)
+            for g in range(SLOTS // NQ):
+                slots = slice(g * NQ, (g + 1) * NQ)
+                product(u_codes[:], u_scales[:], k_pass[:, o, slots], o, 0, slots, False, (o, g) == (1, 3))
 
         neg_max = sb.tile([P, 1], F32, name="neg_max")
         nc.vector.tensor_reduce(neg_max[:], scores[:], mybir.AxisListType.X, ALU.max, negate=True)

@@ -110,7 +110,8 @@ def tile_attend_txlw_topk_kernel(tc, uT, vT, k_words, k_scales, c_words, c_scale
         for o in range(PASSES):
             interleave(u_grouped[o][:], u_raw[o])
 
-        every = slice(0, SLOTS)
+        whole = [slice(0, SLOTS)]
+        pieces = [slice(g * NQ, (g + 1) * NQ) for g in range(SLOTS // NQ)]
         c_picked = sb.tile([P, SLOTS], U32, name="c_picked", align_bytes=64)
         nc.vector.tensor_copy(c_picked[:], cw_pool[:].bitcast(U32).indirect(c_list[:]))
         v_codes, v_scales = quantize(v_grouped[:].rearrange("p o q t -> p (o q t)"), PASSES * NQ, "v")
@@ -121,14 +122,15 @@ def tile_attend_txlw_topk_kernel(tc, uT, vT, k_words, k_scales, c_words, c_scale
             out=warm[:],
             lhsT=v_codes[:, :NQ].bitcast(FP8X4),
             lhsT_scale=v_scales[:, :NQ],
-            rhs=c_picked[:, : SLOTS // 2].bitcast(U16).bitcast(FP4X4),
+            rhs=c_pass[:, 0, :].bitcast(FP4X4),
             rhs_scale=picked_scales[:, 1, :],
             start=True,
             stop=True,
         )
         for o in range(PASSES):
             cols = slice(o * NQ, (o + 1) * NQ)
-            product(v_codes[:, cols], v_scales[:, cols], c_pass[:, o, :], o, 1, every, o == 0, False)
+            for slots in (whole, pieces)[o]:
+                product(v_codes[:, cols], v_scales[:, cols], c_pass[:, o, slots], o, 1, slots, o == 0, False)
 
         half = SLOTS // 2
         k_pass = sb.tile([P, PASSES, SLOTS], U16, name="k_pass", align_bytes=64)
@@ -145,9 +147,8 @@ def tile_attend_txlw_topk_kernel(tc, uT, vT, k_words, k_scales, c_words, c_scale
             )
         for o in range(PASSES):
             u_codes, u_scales = quantize(u_grouped[o][:].rearrange("p q t -> p (q t)"), NQ, "u%d" % o)
-            for g in range(SLOTS // NQ):
-                slots = slice(g * NQ, (g + 1) * NQ)
-                product(u_codes[:], u_scales[:], k_pass[:, o, slots], o, 0, slots, False, (o, g) == (1, 3))
+            for slots in (pieces, whole)[o]:
+                product(u_codes[:], u_scales[:], k_pass[:, o, slots], o, 0, slots, False, o == PASSES - 1)
 
         neg_max = sb.tile([P, 1], F32, name="neg_max")
         nc.vector.tensor_reduce(neg_max[:], scores[:], mybir.AxisListType.X, ALU.max, negate=True)
@@ -156,7 +157,7 @@ def tile_attend_txlw_topk_kernel(tc, uT, vT, k_words, k_scales, c_words, c_scale
         nc.scalar.activation(weights[:], scores[:], ACT.Exp, bias=neg_max[:], scale=1.0, accum_out=row_sum[:])
         inv_sum = sb.tile([P, 1], F32, name="inv_sum")
         nc.vector.reciprocal(inv_sum[:], row_sum[:])
-        split = 320
+        split = 256
         left = sb.tile([P, split], F32, name="left")
         right = sb.tile([P, SLOTS - split], F32, name="right")
         nc.vector.tensor_scalar(left[:], weights[:, :split], inv_sum[:], None, ALU.mult)

@@ -39,33 +39,31 @@ def tile_attend_txlw_topk_kernel(tc, uT, vT, k_words, k_scales, c_words, c_scale
         cs_pool = sb.tile([P, c_cols], U8, name="cs_pool", align_bytes=64)
         kw_pool = sb.tile([P, k_cols], I32, name="kw_pool", align_bytes=64)
         cw_pool = sb.tile([P, c_cols], I32, name="cw_pool", align_bytes=64)
-        picked_scales = sb.tile([P, 2, SLOTS], U8, name="picked_scales", align_bytes=64)
 
-        nc.sync.dma_start(c_list[:], offs2)
-        nc.scalar.dma_start(cs_pool[96:128, :].bitcast(I32), c_scales.rearrange("o f n -> f o n").bitcast(I32))
-        nc.scalar.dma_start(ks_pool[96:128, :].bitcast(I32), k_scales.rearrange("o f n -> f o n").bitcast(I32))
-        nc.scalar.dma_start(cw_pool[:], c_words[0].rearrange("p t b -> p (t b)").bitcast(I32))
-
-        def load_queries(src, o, raw, queue):
+        def load_queries(src, o, raw):
             rows = src[0, o * K_PASS : (o + 1) * K_PASS, :]
-            queue.dma_start(raw[:], rows.rearrange("(p j) q -> p j q", j=PACK))
+            nc.scalar.dma_start(raw, rows.rearrange("(p j) q -> p j q", j=PACK))
             return raw
 
-        v_raw = [
-            load_queries(vT, 0, sb.tile([P, PACK, NQ], F32, name="v_raw0", align_bytes=64), nc.sync),
-        ]
+        nc.sync.dma_start(c_list[:], offs2)
         nc.sync.dma_start(k_list[:], offs)
-        v1_room = held.tile([P, 2 * PACK, NQ], F32, name="v1_room", align_bytes=64, offset=1024)
-        v_raw.append(load_queries(vT, 1, v1_room[:, :PACK], nc.sync))
-        nc.sync.dma_start(kw_pool[:], k_words[0].rearrange("p t b -> p (t b)").bitcast(I32))
+        nc.sync.dma_start(cw_pool[:], c_words[0].rearrange("p t b -> p (t b)").bitcast(I32))
+        nc.scalar.dma_start(cs_pool[96:128, :].bitcast(I32), c_scales.rearrange("o f n -> f o n").bitcast(I32))
+        nc.scalar.dma_start(ks_pool[96:128, :].bitcast(I32), k_scales.rearrange("o f n -> f o n").bitcast(I32))
+        v1_room = held.tile([P, 3 * PACK, NQ], F32, name="v1_room", align_bytes=64, offset=1024)
+        v_raw = [
+            load_queries(vT, 0, sb.tile([P, PACK, NQ], F32, name="v_raw0", align_bytes=64)[:]),
+            load_queries(vT, 1, v1_room[:, :PACK]),
+        ]
+        nc.scalar.dma_start(kw_pool[:], k_words[0].rearrange("p t b -> p (t b)").bitcast(I32))
 
         nc.vector.memset(cs_pool[0:96, :].bitcast(I32), 0)
         nc.gpsimd.memset(ks_pool[0:96, :].bitcast(I32), 0)
 
-        def interleave(grouped, raw):
-            nc.scalar.copy(
+        def interleave(grouped, raw, copy=nc.scalar.copy):
+            copy(
                 grouped.rearrange("p (c i) t -> p c t i", i=4),
-                raw[:].rearrange("p t (c i) -> p c t i", i=4),
+                raw.rearrange("p t (c i) -> p c t i", i=4),
             )
 
         def quantize(grouped, width, name):
@@ -74,20 +72,27 @@ def tile_attend_txlw_topk_kernel(tc, uT, vT, k_words, k_scales, c_words, c_scale
             nc.vector.quantize_mx(out=codes[:].bitcast(FP8X4), scales=scales[:], in_=grouped)
             return codes, scales
 
+        def move_scales(planes, picked):
+            for quad in (0, 2, 1, 3):
+                nc.sync.dma_start(
+                    planes[32 * quad : 32 * quad + 4].bitcast(I32),
+                    picked[96 + 8 * quad : 96 + 8 * quad + 8].bitcast(I32),
+                )
+
         scores = psum.tile([NQ, SLOTS], F32, name="scores")
 
-        def product(codes, scales, words, o, table, slots, start, stop):
+        def product(codes, scales, words, plane, slots, start, stop):
             nc.tensor.matmul_mx(
                 out=scores[:, slots],
                 lhsT=codes.bitcast(FP8X4),
                 lhsT_scale=scales,
                 rhs=words.bitcast(FP4X4),
-                rhs_scale=planes[:, o, table, slots],
+                rhs_scale=plane[:, slots],
                 start=start,
                 stop=stop,
             )
 
-        v_grouped = sb.tile([P, PASSES, NQ, PACK], BF16, name="v_grouped", align_bytes=64)
+        v_grouped = sb.tile([P, PASSES, NQ, PACK], BF16, name="v_grouped", tag="v_grouped_room", align_bytes=64)
         u_grouped = [
             sb.tile([P, NQ, PACK], BF16, name="u_grouped%d" % o, tag="u_grouped%d" % o, align_bytes=64)
             for o in range(PASSES)
@@ -95,23 +100,21 @@ def tile_attend_txlw_topk_kernel(tc, uT, vT, k_words, k_scales, c_words, c_scale
         for o in range(PASSES):
             interleave(v_grouped[:, o], v_raw[o])
 
-        nc.vector.tensor_copy(picked_scales[:, 1, :], cs_pool[:].indirect(c_list[:]))
-        nc.vector.tensor_copy(picked_scales[:, 0, :], ks_pool[:].indirect(k_list[:]))
-        planes = sb.tile([P, PASSES, 2, SLOTS], U8, name="planes", align_bytes=64)
-        for quad in (0, 2, 1, 3):
-            nc.sync.dma_start(
-                planes[32 * quad : 32 * quad + 4].rearrange("p o s n -> p o (s n)").bitcast(I32),
-                picked_scales[96 + 8 * quad : 96 + 8 * quad + 8].rearrange("p s n -> p (s n)").bitcast(I32),
-            )
+        cs_picked = sb.tile([P, SLOTS], U8, name="cs_picked", align_bytes=64)
+        ks_picked = sb.tile([P, SLOTS], U8, name="ks_picked", align_bytes=64)
+        nc.vector.tensor_copy(cs_picked[:], cs_pool[:].indirect(c_list[:]))
+        nc.vector.tensor_copy(ks_picked[:], ks_pool[:].indirect(k_list[:]))
+        c_planes = sb.tile([P, PASSES, SLOTS], U8, name="c_planes", align_bytes=64)
+        move_scales(c_planes, cs_picked)
         u_raw = [
-            load_queries(uT, o, held.tile([P, PACK, NQ], F32, name="u_raw%d" % o, align_bytes=64, offset=4096 * o), nc.scalar)
+            load_queries(uT, o, held.tile([P, PACK, NQ], F32, name="u_raw%d" % o, align_bytes=64, offset=6144 * o)[:])
             for o in range(PASSES)
         ]
-        for o in range(PASSES):
-            interleave(u_grouped[o][:], u_raw[o])
+        share = 48
+        interleave(u_grouped[0][:], u_raw[0])
+        interleave(u_grouped[1][:, :share], u_raw[1][:, :, :share])
 
-        whole = [slice(0, SLOTS)]
-        pieces = [slice(g * NQ, (g + 1) * NQ) for g in range(SLOTS // NQ)]
+        every = slice(0, SLOTS)
         c_picked = sb.tile([P, SLOTS], U32, name="c_picked", align_bytes=64)
         nc.vector.tensor_copy(c_picked[:], cw_pool[:].bitcast(U32).indirect(c_list[:]))
         v_codes, v_scales = quantize(v_grouped[:].rearrange("p o q t -> p (o q t)"), PASSES * NQ, "v")
@@ -122,33 +125,37 @@ def tile_attend_txlw_topk_kernel(tc, uT, vT, k_words, k_scales, c_words, c_scale
             out=warm[:],
             lhsT=v_codes[:, :NQ].bitcast(FP8X4),
             lhsT_scale=v_scales[:, :NQ],
-            rhs=c_pass[:, 0, :].bitcast(FP4X4),
-            rhs_scale=picked_scales[:, 1, :],
+            rhs=c_picked[:, : SLOTS // 2].bitcast(U16).bitcast(FP4X4),
+            rhs_scale=cs_picked[:],
             start=True,
             stop=True,
         )
         for o in range(PASSES):
             cols = slice(o * NQ, (o + 1) * NQ)
-            for slots in (whole, pieces)[o]:
-                product(v_codes[:, cols], v_scales[:, cols], c_pass[:, o, slots], o, 1, slots, o == 0, False)
+            product(v_codes[:, cols], v_scales[:, cols], c_pass[:, o, :], c_planes[:, o], every, o == 0, False)
+
+        k_planes = sb.tile([P, PASSES, SLOTS], U8, name="k_planes", tag="v_grouped_room", align_bytes=64)
+        move_scales(k_planes, ks_picked)
 
         half = SLOTS // 2
-        k_pass = sb.tile([P, PASSES, SLOTS], U16, name="k_pass", align_bytes=64)
-        k_picked = [sb.tile([P, half], U32, name="k_picked%d" % h, tag="k_picked%d" % h, align_bytes=64) for h in range(2)]
+        k_picked = [held.tile([P, half], U32, name="k_picked%d" % h, align_bytes=64, offset=4096 + 1024 * h) for h in range(2)]
         for h in range(2):
             nc.vector.tensor_copy(
                 k_picked[h][:],
                 kw_pool[:].bitcast(U32).indirect(k_list[:, h * half // 16 : (h + 1) * half // 16]),
             )
-        for h in range(2):
-            nc.vector.tensor_copy(
-                k_pass[:, :, h * half : (h + 1) * half],
-                k_picked[h][:].bitcast(U16).rearrange("p (n h) -> p h n", h=2),
-            )
+        pairs = [k_picked[h][:].bitcast(U16).rearrange("p (n h) -> p h n", h=2) for h in range(2)]
+        k_low = sb.tile([P, PASSES, half], U16, name="k_low", align_bytes=64)
+        nc.vector.tensor_copy(k_low[:], pairs[0])
+        interleave(u_grouped[1][:, share:], u_raw[1][:, :, share:], nc.vector.tensor_copy)
         for o in range(PASSES):
             u_codes, u_scales = quantize(u_grouped[o][:].rearrange("p q t -> p (q t)"), NQ, "u%d" % o)
-            for slots in (pieces, whole)[o]:
-                product(u_codes[:], u_scales[:], k_pass[:, o, slots], o, 0, slots, False, o == PASSES - 1)
+            k_high = held.tile([P, half], U16, name="k_high%d" % o, align_bytes=64, offset=7168 * o)
+            nc.vector.tensor_copy(k_high[:], pairs[1][:, o])
+            for g in range(SLOTS // NQ):
+                slots = slice(g * NQ, (g + 1) * NQ)
+                words = (k_low[:, o], k_high[:])[g // 2][:, (g % 2) * NQ : (g % 2 + 1) * NQ]
+                product(u_codes[:], u_scales[:], words, k_planes[:, o], slots, False, (o, g) == (1, 3))
 
         neg_max = sb.tile([P, 1], F32, name="neg_max")
         nc.vector.tensor_reduce(neg_max[:], scores[:], mybir.AxisListType.X, ALU.max, negate=True)

@@ -19,6 +19,12 @@ K_PASS = P * PACK
 PASSES = 2
 NQ = 128
 SLOTS = 512
+HALF = SLOTS // 2
+PIECE = 128
+QUAD = 32
+SCALE_BASE = 96
+SCALAR_ROWS = 48
+KIB = 1024
 FLOPS = 2 * 2 * NQ * SLOTS * PASSES * K_PASS
 
 
@@ -42,25 +48,25 @@ def tile_attend_txlw_topk_kernel(tc, uT, vT, k_words, k_scales, c_words, c_scale
 
         def load_queries(src, o, raw):
             rows = src[0, o * K_PASS : (o + 1) * K_PASS, :]
-            nc.scalar.dma_start(raw, rows.rearrange("(p j) q -> p j q", j=PACK))
+            nc.scalar.dma_start(raw, rows.rearrange("(p t) q -> p t q", t=PACK))
             return raw
 
         nc.sync.dma_start(c_list[:], offs2)
         nc.sync.dma_start(k_list[:], offs)
-        nc.sync.dma_start(cw_pool[:], c_words[0].rearrange("p t b -> p (t b)").bitcast(I32))
-        nc.scalar.dma_start(cs_pool[96:128, :].bitcast(I32), c_scales.rearrange("o f n -> f o n").bitcast(I32))
-        nc.scalar.dma_start(ks_pool[96:128, :].bitcast(I32), k_scales.rearrange("o f n -> f o n").bitcast(I32))
-        v1_room = held.tile([P, 3 * PACK, NQ], F32, name="v1_room", align_bytes=64, offset=1024)
+        nc.sync.dma_start(cw_pool[:], c_words[0].rearrange("p n b -> p (n b)").bitcast(I32))
+        nc.scalar.dma_start(cs_pool[SCALE_BASE:, :].bitcast(I32), c_scales.rearrange("o f n -> f o n").bitcast(I32))
+        nc.scalar.dma_start(ks_pool[SCALE_BASE:, :].bitcast(I32), k_scales.rearrange("o f n -> f o n").bitcast(I32))
+        v1_room = held.tile([P, 3 * PACK, NQ], F32, name="v1_room", align_bytes=64, offset=KIB)
         v_raw = [
-            load_queries(vT, 0, sb.tile([P, PACK, NQ], F32, name="v_raw0", align_bytes=64)[:]),
+            load_queries(vT, 0, sb.tile([P, PACK, NQ], F32, name="v_raw0", tag="v0_room", align_bytes=64)[:]),
             load_queries(vT, 1, v1_room[:, :PACK]),
         ]
-        nc.scalar.dma_start(kw_pool[:], k_words[0].rearrange("p t b -> p (t b)").bitcast(I32))
+        nc.scalar.dma_start(kw_pool[:], k_words[0].rearrange("p n b -> p (n b)").bitcast(I32))
 
-        nc.vector.memset(cs_pool[0:96, :].bitcast(I32), 0)
-        nc.gpsimd.memset(ks_pool[0:96, :].bitcast(I32), 0)
+        nc.vector.memset(cs_pool[:SCALE_BASE, :].bitcast(I32), 0)
+        nc.gpsimd.memset(ks_pool[:SCALE_BASE, :].bitcast(I32), 0)
 
-        def interleave(grouped, raw, copy=nc.scalar.copy):
+        def interleave(grouped, raw, copy):
             copy(
                 grouped.rearrange("p (c i) t -> p c t i", i=4),
                 raw.rearrange("p t (c i) -> p c t i", i=4),
@@ -74,9 +80,10 @@ def tile_attend_txlw_topk_kernel(tc, uT, vT, k_words, k_scales, c_words, c_scale
 
         def move_scales(planes, picked):
             for quad in (0, 2, 1, 3):
+                rows = SCALE_BASE + 4 * PASSES * quad
                 nc.sync.dma_start(
-                    planes[32 * quad : 32 * quad + 4].bitcast(I32),
-                    picked[96 + 8 * quad : 96 + 8 * quad + 8].bitcast(I32),
+                    planes[QUAD * quad : QUAD * quad + 4].bitcast(I32),
+                    picked[rows : rows + 4 * PASSES].bitcast(I32),
                 )
 
         scores = psum.tile([NQ, SLOTS], F32, name="scores")
@@ -92,13 +99,16 @@ def tile_attend_txlw_topk_kernel(tc, uT, vT, k_words, k_scales, c_words, c_scale
                 stop=stop,
             )
 
-        v_grouped = sb.tile([P, PASSES, NQ, PACK], BF16, name="v_grouped", tag="v_grouped_room", align_bytes=64)
+        v_grouped = [
+            sb.tile([P, NQ, PACK], BF16, name="v_grouped0", align_bytes=64),
+            sb.tile([P, NQ, PACK], BF16, name="v_grouped1", tag="v_grouped_room", align_bytes=64),
+        ]
         u_grouped = [
             sb.tile([P, NQ, PACK], BF16, name="u_grouped%d" % o, tag="u_grouped%d" % o, align_bytes=64)
             for o in range(PASSES)
         ]
         for o in range(PASSES):
-            interleave(v_grouped[:, o], v_raw[o])
+            interleave(v_grouped[o][:], v_raw[o], nc.scalar.copy)
 
         cs_picked = sb.tile([P, SLOTS], U8, name="cs_picked", align_bytes=64)
         ks_picked = sb.tile([P, SLOTS], U8, name="ks_picked", align_bytes=64)
@@ -106,56 +116,64 @@ def tile_attend_txlw_topk_kernel(tc, uT, vT, k_words, k_scales, c_words, c_scale
         nc.vector.tensor_copy(ks_picked[:], ks_pool[:].indirect(k_list[:]))
         c_planes = sb.tile([P, PASSES, SLOTS], U8, name="c_planes", align_bytes=64)
         move_scales(c_planes, cs_picked)
+
         u_raw = [
-            load_queries(uT, o, held.tile([P, PACK, NQ], F32, name="u_raw%d" % o, align_bytes=64, offset=6144 * o)[:])
+            load_queries(uT, o, held.tile([P, PACK, NQ], F32, name="u_raw%d" % o, align_bytes=64, offset=6 * KIB * o)[:])
             for o in range(PASSES)
         ]
-        share = 48
-        interleave(u_grouped[0][:], u_raw[0])
-        interleave(u_grouped[1][:, :share], u_raw[1][:, :, :share])
+        interleave(u_grouped[0][:], u_raw[0], nc.scalar.copy)
+        interleave(u_grouped[1][:, :SCALAR_ROWS], u_raw[1][:, :, :SCALAR_ROWS], nc.scalar.copy)
 
         every = slice(0, SLOTS)
         c_picked = sb.tile([P, SLOTS], U32, name="c_picked", align_bytes=64)
         nc.vector.tensor_copy(c_picked[:], cw_pool[:].bitcast(U32).indirect(c_list[:]))
-        v_codes, v_scales = quantize(v_grouped[:].rearrange("p o q t -> p (o q t)"), PASSES * NQ, "v")
-        c_pass = held.tile([P, PASSES, SLOTS], U16, name="c_pass", align_bytes=64, offset=2048)
-        nc.vector.tensor_copy(c_pass[:], c_picked[:].bitcast(U16).rearrange("p (n h) -> p h n", h=2))
+        c_pairs = c_picked[:].bitcast(U16).rearrange("p (n o) -> p o n", o=PASSES)
+        c_pass = [
+            sb.tile([P, SLOTS], U16, name="c_pass0", tag="v0_room", align_bytes=64),
+            held.tile([P, SLOTS], U16, name="c_pass1", align_bytes=64, offset=2 * KIB),
+        ]
         warm = psum.tile([NQ, SLOTS], F32, name="warm")
-        nc.tensor.matmul_mx(
-            out=warm[:],
-            lhsT=v_codes[:, :NQ].bitcast(FP8X4),
-            lhsT_scale=v_scales[:, :NQ],
-            rhs=c_picked[:, : SLOTS // 2].bitcast(U16).bitcast(FP4X4),
-            rhs_scale=cs_picked[:],
-            start=True,
-            stop=True,
-        )
         for o in range(PASSES):
-            cols = slice(o * NQ, (o + 1) * NQ)
-            product(v_codes[:, cols], v_scales[:, cols], c_pass[:, o, :], c_planes[:, o], every, o == 0, False)
+            v_codes, v_scales = quantize(v_grouped[o][:].rearrange("p q t -> p (q t)"), NQ, "v%d" % o)
+            if o == 0:
+                nc.tensor.matmul_mx(
+                    out=warm[:],
+                    lhsT=v_codes[:].bitcast(FP8X4),
+                    lhsT_scale=v_scales[:],
+                    rhs=c_picked[:, :HALF].bitcast(U16).bitcast(FP4X4),
+                    rhs_scale=cs_picked[:],
+                    start=True,
+                    stop=True,
+                )
+            nc.vector.tensor_copy(c_pass[o][:], c_pairs[:, o])
+            product(v_codes[:], v_scales[:], c_pass[o][:], c_planes[:, o], every, o == 0, False)
 
         k_planes = sb.tile([P, PASSES, SLOTS], U8, name="k_planes", tag="v_grouped_room", align_bytes=64)
         move_scales(k_planes, ks_picked)
 
-        half = SLOTS // 2
-        k_picked = [held.tile([P, half], U32, name="k_picked%d" % h, align_bytes=64, offset=4096 + 1024 * h) for h in range(2)]
+        k_picked = [
+            held.tile([P, HALF], U32, name="k_picked%d" % h, align_bytes=64, offset=(4 + h) * KIB) for h in range(2)
+        ]
         for h in range(2):
             nc.vector.tensor_copy(
                 k_picked[h][:],
-                kw_pool[:].bitcast(U32).indirect(k_list[:, h * half // 16 : (h + 1) * half // 16]),
+                kw_pool[:].bitcast(U32).indirect(k_list[:, h * HALF // 16 : (h + 1) * HALF // 16]),
             )
-        pairs = [k_picked[h][:].bitcast(U16).rearrange("p (n h) -> p h n", h=2) for h in range(2)]
-        k_low = sb.tile([P, PASSES, half], U16, name="k_low", align_bytes=64)
-        nc.vector.tensor_copy(k_low[:], pairs[0])
-        interleave(u_grouped[1][:, share:], u_raw[1][:, :, share:], nc.vector.tensor_copy)
+        k_pairs = [k_picked[h][:].bitcast(U16).rearrange("p (n o) -> p o n", o=PASSES) for h in range(2)]
+        k_lower = sb.tile([P, PASSES, HALF], U16, name="k_lower", align_bytes=64)
+        nc.vector.tensor_copy(k_lower[:], k_pairs[0])
+        interleave(u_grouped[1][:, SCALAR_ROWS:], u_raw[1][:, :, SCALAR_ROWS:], nc.vector.tensor_copy)
+        pieces = SLOTS // PIECE
         for o in range(PASSES):
             u_codes, u_scales = quantize(u_grouped[o][:].rearrange("p q t -> p (q t)"), NQ, "u%d" % o)
-            k_high = held.tile([P, half], U16, name="k_high%d" % o, align_bytes=64, offset=7168 * o)
-            nc.vector.tensor_copy(k_high[:], pairs[1][:, o])
-            for g in range(SLOTS // NQ):
-                slots = slice(g * NQ, (g + 1) * NQ)
-                words = (k_low[:, o], k_high[:])[g // 2][:, (g % 2) * NQ : (g % 2 + 1) * NQ]
-                product(u_codes[:], u_scales[:], words, k_planes[:, o], slots, False, (o, g) == (1, 3))
+            k_upper = held.tile([P, HALF], U16, name="k_upper%d" % o, align_bytes=64, offset=7 * KIB * o)
+            nc.vector.tensor_copy(k_upper[:], k_pairs[1][:, o])
+            for g in range(pieces):
+                h, first = divmod(g * PIECE, HALF)
+                words = (k_lower[:, o], k_upper[:])[h][:, first : first + PIECE]
+                slots = slice(g * PIECE, (g + 1) * PIECE)
+                last = o == PASSES - 1 and g == pieces - 1
+                product(u_codes[:], u_scales[:], words, k_planes[:, o], slots, False, last)
 
         neg_max = sb.tile([P, 1], F32, name="neg_max")
         nc.vector.tensor_reduce(neg_max[:], scores[:], mybir.AxisListType.X, ALU.max, negate=True)
@@ -164,10 +182,9 @@ def tile_attend_txlw_topk_kernel(tc, uT, vT, k_words, k_scales, c_words, c_scale
         nc.scalar.activation(weights[:], scores[:], ACT.Exp, bias=neg_max[:], scale=1.0, accum_out=row_sum[:])
         inv_sum = sb.tile([P, 1], F32, name="inv_sum")
         nc.vector.reciprocal(inv_sum[:], row_sum[:])
-        split = 256
-        left = sb.tile([P, split], F32, name="left")
-        right = sb.tile([P, SLOTS - split], F32, name="right")
-        nc.vector.tensor_scalar(left[:], weights[:, :split], inv_sum[:], None, ALU.mult)
-        nc.sync.dma_start(out[0, :, :split], left[:])
-        nc.scalar.activation(right[:], weights[:, split:], ACT.Copy, scale=inv_sum[:])
-        nc.scalar.dma_start(out[0, :, split:], right[:])
+        left = sb.tile([P, HALF], F32, name="left")
+        right = sb.tile([P, HALF], F32, name="right")
+        nc.vector.tensor_scalar(left[:], weights[:, :HALF], inv_sum[:], None, ALU.mult)
+        nc.sync.dma_start(out[0, :, :HALF], left[:])
+        nc.scalar.activation(right[:], weights[:, HALF:], ACT.Copy, scale=inv_sum[:])
+        nc.scalar.dma_start(out[0, :, HALF:], right[:])

@@ -132,19 +132,8 @@ def tile_attend_txlw_topk_kernel(tc, uT, vT, k_words, k_scales, c_words, c_scale
             sb.tile([P, SLOTS], U16, name="c_pass0", tag="v0_room", align_bytes=64),
             held.tile([P, SLOTS], U16, name="c_pass1", align_bytes=64, offset=2 * KIB),
         ]
-        warm = psum.tile([NQ, SLOTS], F32, name="warm")
         for o in range(PASSES):
             v_codes, v_scales = quantize(v_grouped[o][:].rearrange("p q t -> p (q t)"), NQ, "v%d" % o)
-            if o == 0:
-                nc.tensor.matmul_mx(
-                    out=warm[:],
-                    lhsT=v_codes[:].bitcast(FP8X4),
-                    lhsT_scale=v_scales[:],
-                    rhs=c_picked[:, :HALF].bitcast(U16).bitcast(FP4X4),
-                    rhs_scale=cs_picked[:],
-                    start=True,
-                    stop=True,
-                )
             nc.vector.tensor_copy(c_pass[o][:], c_pairs[:, o])
             product(v_codes[:], v_scales[:], c_pass[o][:], c_planes[:, o], every, o == 0, False)
 

@@ -22,7 +22,8 @@ SLOTS = 512
 HALF = SLOTS // 2
 PIECE = 128
 QUAD = 32
-SCALE_BASE = 96
+C_BASE = 96
+K_BASE = 32
 SCALAR_ROWS = 48
 KIB = 1024
 FLOPS = 2 * 2 * NQ * SLOTS * PASSES * K_PASS
@@ -54,17 +55,19 @@ def tile_attend_txlw_topk_kernel(tc, uT, vT, k_words, k_scales, c_words, c_scale
         nc.sync.dma_start(c_list[:], offs2)
         nc.sync.dma_start(k_list[:], offs)
         nc.sync.dma_start(cw_pool[:], c_words[0].rearrange("p n b -> p (n b)").bitcast(I32))
-        nc.scalar.dma_start(cs_pool[SCALE_BASE:, :].bitcast(I32), c_scales.rearrange("o f n -> f o n").bitcast(I32))
-        nc.scalar.dma_start(ks_pool[SCALE_BASE:, :].bitcast(I32), k_scales.rearrange("o f n -> f o n").bitcast(I32))
+        nc.scalar.dma_start(cs_pool[C_BASE : C_BASE + QUAD, :].bitcast(I32), c_scales.rearrange("o f n -> f o n").bitcast(I32))
+        nc.scalar.dma_start(ks_pool[K_BASE : K_BASE + QUAD, :].bitcast(I32), k_scales.rearrange("o f n -> f o n").bitcast(I32))
         v1_room = held.tile([P, 3 * PACK, NQ], F32, name="v1_room", align_bytes=64, offset=KIB)
+        v0_room = held.tile([P, 3 * PACK, NQ], F32, name="v0_room", align_bytes=64, offset=8 * KIB)
         v_raw = [
-            load_queries(vT, 0, sb.tile([P, PACK, NQ], F32, name="v_raw0", tag="v0_room", align_bytes=64)[:]),
+            load_queries(vT, 0, v0_room[:, :PACK]),
             load_queries(vT, 1, v1_room[:, :PACK]),
         ]
         nc.scalar.dma_start(kw_pool[:], k_words[0].rearrange("p n b -> p (n b)").bitcast(I32))
 
-        nc.vector.memset(cs_pool[:SCALE_BASE, :].bitcast(I32), 0)
-        nc.gpsimd.memset(ks_pool[:SCALE_BASE, :].bitcast(I32), 0)
+        nc.vector.memset(cs_pool[:C_BASE, :].bitcast(I32), 0)
+        nc.vector.memset(ks_pool[:K_BASE, :].bitcast(I32), 0)
+        nc.vector.memset(ks_pool[K_BASE + QUAD :, :].bitcast(I32), 0)
 
         def interleave(grouped, raw, copy):
             copy(
@@ -78,9 +81,9 @@ def tile_attend_txlw_topk_kernel(tc, uT, vT, k_words, k_scales, c_words, c_scale
             nc.vector.quantize_mx(out=codes[:].bitcast(FP8X4), scales=scales[:], in_=grouped)
             return codes, scales
 
-        def move_scales(planes, picked):
+        def move_scales(planes, picked, base):
             for quad in (0, 2, 1, 3):
-                rows = SCALE_BASE + 4 * PASSES * quad
+                rows = base + 4 * PASSES * quad
                 nc.sync.dma_start(
                     planes[QUAD * quad : QUAD * quad + 4].bitcast(I32),
                     picked[rows : rows + 4 * PASSES].bitcast(I32),
@@ -115,10 +118,10 @@ def tile_attend_txlw_topk_kernel(tc, uT, vT, k_words, k_scales, c_words, c_scale
         nc.vector.tensor_copy(cs_picked[:], cs_pool[:].indirect(c_list[:]))
         nc.vector.tensor_copy(ks_picked[:], ks_pool[:].indirect(k_list[:]))
         c_planes = sb.tile([P, PASSES, SLOTS], U8, name="c_planes", align_bytes=64)
-        move_scales(c_planes, cs_picked)
+        move_scales(c_planes, cs_picked, C_BASE)
 
         u_raw = [
-            load_queries(uT, o, held.tile([P, PACK, NQ], F32, name="u_raw%d" % o, align_bytes=64, offset=6 * KIB * o)[:])
+            load_queries(uT, o, held.tile([P, PACK, NQ], F32, name="u_raw%d" % o, align_bytes=64, offset=(10 + 2 * o) * KIB)[:])
             for o in range(PASSES)
         ]
         interleave(u_grouped[0][:], u_raw[0], nc.scalar.copy)
@@ -129,7 +132,7 @@ def tile_attend_txlw_topk_kernel(tc, uT, vT, k_words, k_scales, c_words, c_scale
         nc.vector.tensor_copy(c_picked[:], cw_pool[:].bitcast(U32).indirect(c_list[:]))
         c_pairs = c_picked[:].bitcast(U16).rearrange("p (n o) -> p o n", o=PASSES)
         c_pass = [
-            sb.tile([P, SLOTS], U16, name="c_pass0", tag="v0_room", align_bytes=64),
+            held.tile([P, SLOTS], U16, name="c_pass0", align_bytes=64, offset=8 * KIB),
             held.tile([P, SLOTS], U16, name="c_pass1", align_bytes=64, offset=2 * KIB),
         ]
         for o in range(PASSES):
@@ -138,7 +141,7 @@ def tile_attend_txlw_topk_kernel(tc, uT, vT, k_words, k_scales, c_words, c_scale
             product(v_codes[:], v_scales[:], c_pass[o][:], c_planes[:, o], every, o == 0, False)
 
         k_planes = sb.tile([P, PASSES, SLOTS], U8, name="k_planes", tag="v_grouped_room", align_bytes=64)
-        move_scales(k_planes, ks_picked)
+        move_scales(k_planes, ks_picked, K_BASE)
 
         k_picked = [
             held.tile([P, HALF], U32, name="k_picked%d" % h, align_bytes=64, offset=(4 + h) * KIB) for h in range(2)
@@ -155,7 +158,7 @@ def tile_attend_txlw_topk_kernel(tc, uT, vT, k_words, k_scales, c_words, c_scale
         pieces = SLOTS // PIECE
         for o in range(PASSES):
             u_codes, u_scales = quantize(u_grouped[o][:].rearrange("p q t -> p (q t)"), NQ, "u%d" % o)
-            k_upper = held.tile([P, HALF], U16, name="k_upper%d" % o, align_bytes=64, offset=7 * KIB * o)
+            k_upper = held.tile([P, HALF], U16, name="k_upper%d" % o, align_bytes=64, offset=(10 + 2 * o) * KIB)
             nc.vector.tensor_copy(k_upper[:], k_pairs[1][:, o])
             for g in range(pieces):
                 h, first = divmod(g * PIECE, HALF)

from contextlib import ExitStack

import concourse.mybir as mybir

F32 = mybir.dt.float32
BF16 = mybir.dt.bfloat16
I32 = mybir.dt.int32
U32 = mybir.dt.uint32
U16 = mybir.dt.uint16
U8 = mybir.dt.uint8
FP8X4 = mybir.dt.float8_e4m3fn_x4
FP4X4 = mybir.dt.float4_e2m1fn_x4
ACT = mybir.ActivationFunctionType
ALU = mybir.AluOpType

P = 128
PACK = 4
K_PASS = P * PACK
PASSES = 2
NQ = 128
SLOTS = 512
HALF = SLOTS // 2
PIECE = 128
QUAD = 32
C_BASE = 96
K_BASE = 32
SCALAR_ROWS = 48
KIB = 1024
FLOPS = 2 * 2 * NQ * SLOTS * PASSES * K_PASS


def tile_attend_txlw_topk_kernel(tc, uT, vT, k_words, k_scales, c_words, c_scales, offs, offs2, out):
    nc = tc.nc
    with ExitStack() as ctx:
        lists = ctx.enter_context(tc.tile_pool(name="lists", bufs=1))
        sb = ctx.enter_context(tc.tile_pool(name="sb", bufs=1))
        held = ctx.enter_context(tc.tile_pool(name="held", bufs=1))
        psum = ctx.enter_context(tc.psum_pool(name="psum", bufs=1))

        k_list = lists.tile([P, SLOTS // 16], U16, name="k_list")
        c_list = lists.tile([P, SLOTS // 16], U16, name="c_list")
        k_cols = k_scales.shape[2]
        c_cols = c_scales.shape[2]

        ks_pool = sb.tile([P, k_cols], U8, name="ks_pool", align_bytes=64)
        cs_pool = sb.tile([P, c_cols], U8, name="cs_pool", align_bytes=64)
        kw_pool = sb.tile([P, k_cols], I32, name="kw_pool", align_bytes=64)
        cw_pool = sb.tile([P, c_cols], I32, name="cw_pool", align_bytes=64)

        def load_queries(src, o, raw):
            rows = src[0, o * K_PASS : (o + 1) * K_PASS, :]
            nc.scalar.dma_start(raw, rows.rearrange("(p t) q -> p t q", t=PACK))
            return raw

        nc.sync.dma_start(c_list[:], offs2)
        nc.sync.dma_start(k_list[:], offs)
        nc.sync.dma_start(cw_pool[:], c_words[0].rearrange("p n b -> p (n b)").bitcast(I32))
        nc.scalar.dma_start(cs_pool[C_BASE : C_BASE + QUAD, :].bitcast(I32), c_scales.rearrange("o f n -> f o n").bitcast(I32))
        nc.scalar.dma_start(ks_pool[K_BASE : K_BASE + QUAD, :].bitcast(I32), k_scales.rearrange("o f n -> f o n").bitcast(I32))
        v1_room = held.tile([P, 3 * PACK, NQ], F32, name="v1_room", align_bytes=64, offset=KIB)
        v0_room = held.tile([P, 3 * PACK, NQ], F32, name="v0_room", align_bytes=64, offset=8 * KIB)
        v_raw = [
            load_queries(vT, 0, v0_room[:, :PACK]),
            load_queries(vT, 1, v1_room[:, :PACK]),
        ]
        nc.scalar.dma_start(kw_pool[:], k_words[0].rearrange("p n b -> p (n b)").bitcast(I32))

        nc.vector.memset(cs_pool[:C_BASE, :].bitcast(I32), 0)
        nc.vector.memset(ks_pool[:K_BASE, :].bitcast(I32), 0)
        nc.vector.memset(ks_pool[K_BASE + QUAD :, :].bitcast(I32), 0)

        def interleave(grouped, raw, copy):
            copy(
                grouped.rearrange("p (c i) t -> p c t i", i=4),
                raw.rearrange("p t (c i) -> p c t i", i=4),
            )

        def quantize(grouped, width, name):
            codes = sb.tile([P, width], U32, name=name + "_codes", align_bytes=64)
            scales = sb.tile([P, width], U8, name=name + "_scales", align_bytes=64)
            nc.vector.quantize_mx(out=codes[:].bitcast(FP8X4), scales=scales[:], in_=grouped)
            return codes, scales

        def move_scales(planes, picked, base):
            for quad in (0, 2, 1, 3):
                rows = base + 4 * PASSES * quad
                nc.sync.dma_start(
                    planes[QUAD * quad : QUAD * quad + 4].bitcast(I32),
                    picked[rows : rows + 4 * PASSES].bitcast(I32),
                )

        scores = psum.tile([NQ, SLOTS], F32, name="scores")

        def product(codes, scales, words, plane, slots, start, stop):
            nc.tensor.matmul_mx(
                out=scores[:, slots],
                lhsT=codes.bitcast(FP8X4),
                lhsT_scale=scales,
                rhs=words.bitcast(FP4X4),
                rhs_scale=plane[:, slots],
                start=start,
                stop=stop,
            )

        v_grouped = [
            sb.tile([P, NQ, PACK], BF16, name="v_grouped0", align_bytes=64),
            sb.tile([P, NQ, PACK], BF16, name="v_grouped1", tag="v_grouped_room", align_bytes=64),
        ]
        u_grouped = [
            sb.tile([P, NQ, PACK], BF16, name="u_grouped%d" % o, tag="u_grouped%d" % o, align_bytes=64)
            for o in range(PASSES)
        ]
        for o in range(PASSES):
            interleave(v_grouped[o][:], v_raw[o], nc.scalar.copy)

        cs_picked = sb.tile([P, SLOTS], U8, name="cs_picked", align_bytes=64)
        ks_picked = sb.tile([P, SLOTS], U8, name="ks_picked", align_bytes=64)
        nc.vector.tensor_copy(cs_picked[:], cs_pool[:].indirect(c_list[:]))
        nc.vector.tensor_copy(ks_picked[:], ks_pool[:].indirect(k_list[:]))
        c_planes = sb.tile([P, PASSES, SLOTS], U8, name="c_planes", align_bytes=64)
        move_scales(c_planes, cs_picked, C_BASE)

        u_raw = [
            load_queries(uT, o, held.tile([P, PACK, NQ], F32, name="u_raw%d" % o, align_bytes=64, offset=(10 + 2 * o) * KIB)[:])
            for o in range(PASSES)
        ]
        interleave(u_grouped[0][:], u_raw[0], nc.scalar.copy)
        interleave(u_grouped[1][:, :SCALAR_ROWS], u_raw[1][:, :, :SCALAR_ROWS], nc.scalar.copy)

        every = slice(0, SLOTS)
        c_picked = sb.tile([P, SLOTS], U32, name="c_picked", align_bytes=64)
        nc.vector.tensor_copy(c_picked[:], cw_pool[:].bitcast(U32).indirect(c_list[:]))
        c_pairs = c_picked[:].bitcast(U16).rearrange("p (n o) -> p o n", o=PASSES)
        c_pass = [
            held.tile([P, SLOTS], U16, name="c_pass0", align_bytes=64, offset=8 * KIB),
            held.tile([P, SLOTS], U16, name="c_pass1", align_bytes=64, offset=2 * KIB),
        ]
        for o in range(PASSES):
            v_codes, v_scales = quantize(v_grouped[o][:].rearrange("p q t -> p (q t)"), NQ, "v%d" % o)
            nc.vector.tensor_copy(c_pass[o][:], c_pairs[:, o])
            product(v_codes[:], v_scales[:], c_pass[o][:], c_planes[:, o], every, o == 0, False)

        k_planes = sb.tile([P, PASSES, SLOTS], U8, name="k_planes", tag="v_grouped_room", align_bytes=64)
        move_scales(k_planes, ks_picked, K_BASE)

        k_picked = [
            held.tile([P, HALF], U32, name="k_picked%d" % h, align_bytes=64, offset=(4 + h) * KIB) for h in range(2)
        ]
        for h in range(2):
            nc.vector.tensor_copy(
                k_picked[h][:],
                kw_pool[:].bitcast(U32).indirect(k_list[:, h * HALF // 16 : (h + 1) * HALF // 16]),
            )
        k_pairs = [k_picked[h][:].bitcast(U16).rearrange("p (n o) -> p o n", o=PASSES) for h in range(2)]
        k_lower = sb.tile([P, PASSES, HALF], U16, name="k_lower", align_bytes=64)
        nc.vector.tensor_copy(k_lower[:], k_pairs[0])
        interleave(u_grouped[1][:, SCALAR_ROWS:], u_raw[1][:, :, SCALAR_ROWS:], nc.vector.tensor_copy)
        pieces = SLOTS // PIECE
        for o in range(PASSES):
            u_codes, u_scales = quantize(u_grouped[o][:].rearrange("p q t -> p (q t)"), NQ, "u%d" % o)
            k_upper = held.tile([P, HALF], U16, name="k_upper%d" % o, align_bytes=64, offset=(10 + 2 * o) * KIB)
            nc.vector.tensor_copy(k_upper[:], k_pairs[1][:, o])
            for g in range(pieces):
                h, first = divmod(g * PIECE, HALF)
                words = (k_lower[:, o], k_upper[:])[h][:, first : first + PIECE]
                slots = slice(g * PIECE, (g + 1) * PIECE)
                last = o == PASSES - 1 and g == pieces - 1
                product(u_codes[:], u_scales[:], words, k_planes[:, o], slots, False, last)

        neg_max = sb.tile([P, 1], F32, name="neg_max")
        nc.vector.tensor_reduce(neg_max[:], scores[:], mybir.AxisListType.X, ALU.max, negate=True)
        weights = sb.tile([P, SLOTS], F32, name="weights")
        row_sum = sb.tile([P, 1], F32, name="row_sum")
        nc.scalar.activation(weights[:], scores[:], ACT.Exp, bias=neg_max[:], scale=1.0, accum_out=row_sum[:])
        inv_sum = sb.tile([P, 1], F32, name="inv_sum")
        nc.vector.reciprocal(inv_sum[:], row_sum[:])
        left = sb.tile([P, HALF], F32, name="left")
        right = sb.tile([P, HALF], F32, name="right")
        nc.vector.tensor_scalar(left[:], weights[:, :HALF], inv_sum[:], None, ALU.mult)
        nc.sync.dma_start(out[0, :, :HALF], left[:])
        nc.scalar.activation(right[:], weights[:, HALF:], ACT.Copy, scale=inv_sum[:])
        nc.scalar.dma_start(out[0, :, HALF:], right[:])
